import numpy as np, ml_dtypes
CORES = [8,11,14,16,19,22,24,27,30]
N = 9
R, TK = 16, 256
def setup_inputs(rng):
    v = (rng.standard_normal((N, 128, R), dtype=np.float32) / np.float32(np.sqrt(128 * N))).astype(ml_dtypes.bfloat16)
    return {"x": rng.standard_normal((N, 128, TK), dtype=np.float32).astype(ml_dtypes.bfloat16), "v": v, "vt": v.transpose(0, 2, 1).copy()}
def setup_inputs_big(rng):
    d = setup_inputs(rng)
    for k in ("x",): d[k] = (d[k].astype(np.float32) * 1048576.0).astype(d[k].dtype)
    return d
def setup_inputs_small(rng):
    d = setup_inputs(rng)
    for k in ("x",): d[k] = (d[k].astype(np.float32) * (1 / 1048576.0)).astype(d[k].dtype)
    return d
def setup_inputs_apart(rng):
    d = setup_inputs(rng)
    f = (10.0 ** rng.permutation(np.linspace(-1.5, 1.5, N))).astype(np.float32).reshape(N, 1, 1)
    for k in ("x",): d[k] = (d[k].astype(np.float32) * f).astype(d[k].dtype)
    return d
def reference(x, v, vt):
    X, V, VT = x.astype(np.float64), v.astype(np.float64), vt.astype(np.float64)
    t = sum(V[j].T @ X[j] for j in range(N))
    return {"y": np.stack([X[r] - 2.0 * (VT[r].T @ t) for r in range(N)]).astype(ml_dtypes.bfloat16)}

from concourse.bass import DstId, RemoteDMATransfer
from concourse.mybir import AluOpType

N = 9
RK = 16
NB = 8
BW = 32
NENG = 8

SCRATCH = {
    "xs": ("sbuf", [128, 256], "bfloat16"),
    "q": ("sbuf", [128, 256], "bfloat16"),
    "w": ("sbuf", [128, NB * 128], "bfloat16"),
    "two": ("sbuf", [128, BW], "float32"),
    "p": ("sbuf", [128, N * BW], "bfloat16"),
    "r": ("sbuf", [128, N * BW], "bfloat16"),
    "ys": ("sbuf", [128, 256], "bfloat16"),
    "pp": ("psum", [128, 512], "float32"),
    "acc": ("psum", [128, 512], "float32"),
}
SEMAPHORES = ["ldx", "ldv", "ldw", "fq", "f2", "fw", "m1", "m2", "pr", "a1", "snt", "fin", "st"] + [
    "s%d" % i for i in range(N)]


def _hops(topo, a, b):
    return 1 if (topo.mates(a, b) or topo.same_plane(a, b)) else 2


def _plan(cores, topo):
    plan = {}
    for ch in sorted(set(topo.chip(c) for c in cores)):
        mine = [c for c in cores if topo.chip(c) == ch]
        dests = [d for d in cores if topo.chip(d) != ch]
        best = None
        for code in range(len(mine) ** len(dests)):
            pick, k = [], code
            for _ in dests:
                pick.append(mine[k % len(mine)])
                k //= len(mine)
            if not all(topo.may_write(s, d) for s, d in zip(pick, dests)):
                continue
            load = max(pick.count(s) for s in mine)
            cross = sum(1 for s, d in zip(pick, dests) if topo.die(s) != topo.die(d))
            if best is None or (load, cross, code) < best[0]:
                best = ((load, cross, code), pick)
        for s in mine:
            mylist = [d for s2, d in zip(best[1], dests) if s2 == s]
            plan[s] = sorted(mylist, key=lambda d: (-_hops(topo, ch, topo.chip(d)), d))
    return plan


def _engines(mask, n):
    out, bit, k = 0, 1, 0
    while k < n:
        if mask & bit:
            out |= bit
            k += 1
        bit <<= 1
    return out


def _dst(topo, c):
    rid, pid, _ = topo.addr(c)
    return DstId(rid=rid, pnc=pid)


def rank_program(g, core, T, topo):
    rank = T.rank_of(core)
    if rank is None:
        return
    cores = list(T.cores)
    sem = T.sem
    te, ve = g.tensor, g.vector
    chip = topo.chip(core)
    peers = [c for c in cores if topo.chip(c) == chip and c != core]
    plan = _plan(cores, topo)
    far = plan[core]
    feeders = sorted([s for s in cores if core in plan[s]],
                     key=lambda s: (_hops(topo, topo.chip(s), chip), len(plan[s]), s))
    allowed = -1
    for d in peers + far:
        allowed &= topo.mask(core, d)
    eng = _engines(allowed, NENG)

    def slot(buf, rk):
        return buf[:, BW * rk:BW * (rk + 1)]

    g.sync.dma_start(T.xs[:, :], T.x[:, :]).then_inc(sem.ldx, 16)
    g.scalar.dma_start(T.q[:, 112:128], T.v[:, :]).then_inc(sem.ldv, 16)
    ve.memset(T.q[:, 0:112], 0.0).then_inc(sem.fq, 1)
    ve.memset(T.q[:, 128:256], 0.0).then_inc(sem.fq, 1)
    ve.memset(T.two[:, :], 2.0).then_inc(sem.f2, 1)
    ve.memset(T.w[:, :], 0.0).then_inc(sem.fw, 1)
    g.sync.wait_ge(sem.fw, 1)
    g.scalar.wait_ge(sem.fw, 1)
    for b in range(NB):
        dq = g.sync if b % 2 == 0 else g.scalar
        dq.dma_start(T.w[RK * b:RK * (b + 1), 128 * b:128 * (b + 1)], T.vt[:, :]).then_inc(sem.ldw, 16)

    te.wait_ge(sem.fq, 2)
    te.wait_ge(sem.ldv, 16)
    te.wait_ge(sem.ldx, 16)
    for b in range(NB):
        te.matmul(T.pp[:, 0:BW], T.q[:, 112 - RK * b:240 - RK * b], T.xs[:, BW * b:BW * (b + 1)],
                  b == 0, b == NB - 1).then_inc(sem.m1, 1)
    ve.wait_ge(sem.f2, 1)
    ve.wait_ge(sem.m1, NB)
    ve.tensor_tensor(slot(T.p, rank), T.pp[:, 0:BW], T.two[:, :], AluOpType.mult).then_inc(sem.pr, 1)

    g.wait_ge(sem.pr, 1)
    g.remote_dma_fused([RemoteDMATransfer(
        dst_ids=[_dst(topo, d) for d in peers], dma_engine_mask=eng, remote_sem=sem.a1,
        srcs=[slot(T.p, rank)], dsts=[slot(T.p, rank) for _ in peers], alu_op=0)], local_sem=sem.snt)
    sent = NENG

    if far:
        g.wait_ge(sem.a1, NENG * len(peers))
        g.remote_dma_fused([RemoteDMATransfer(
            dst_ids=[_dst(topo, d) for d in far], dma_engine_mask=eng, remote_sem=sem["s%d" % rank],
            srcs=[slot(T.p, T.rank_of(c)) for c in [core] + peers], dsts=[slot(T.r, rank) for _ in far],
            alu_op=1)], local_sem=sem.snt)
        sent += NENG

    te.matmul(T.acc[:, 0:256], T.q[:, 128:256], T.xs[:, :], True, False).then_inc(sem.m2, 1)
    done = 1
    te.wait_ge(sem.ldw, 16 * NB)
    te.wait_ge(sem.pr, 1)
    groups = [(None, [slot(T.p, rank)]),
              ((sem.a1, NENG * len(peers)), [slot(T.p, T.rank_of(c)) for c in peers])]
    groups += [((sem["s%d" % T.rank_of(s)], NENG), [slot(T.r, T.rank_of(s))]) for s in feeders]
    for gi, (wait, srcs) in enumerate(groups):
        if wait is not None:
            te.wait_ge(wait[0], wait[1])
        for si, src in enumerate(srcs):
            for b in range(NB):
                last = gi == len(groups) - 1 and si == len(srcs) - 1 and b == NB - 1
                te.matmul(T.acc[:, BW * b:BW * (b + 1)], T.w[:, 128 * b:128 * (b + 1)], src,
                          False, last).then_inc(sem.m2, 1)
                done += 1

    ve.wait_ge(sem.ldx, 16)
    ve.wait_ge(sem.m2, done)
    ve.tensor_tensor(T.ys[:, :], T.xs[:, :], T.acc[:, 0:256], AluOpType.subtract).then_inc(sem.fin, 1)
    g.sync.wait_ge(sem.fin, 1)
    g.sync.dma_start(T.y[:, :], T.ys[:, :]).then_inc(sem.st, 16)
    g.sync.wait_ge(sem.st, 16)
    g.wait_ge(sem.snt, sent)
